import numpy as np
import ml_dtypes


def mxq(x, axis, fmt="e4m3"):
    dtype, down = {"e4m3": (ml_dtypes.float8_e4m3fn, 7), "e5m2": (ml_dtypes.float8_e5m2, 14)}[fmt]
    v = np.moveaxis(np.asarray(x, np.float32).astype(ml_dtypes.bfloat16).astype(np.float64), axis, -1)
    blocks = v.reshape(v.shape[:-1] + (-1, 32))
    amax = np.abs(blocks).max(-1, keepdims=True)
    byte = np.maximum(np.where(amax > 0, np.frexp(amax)[1] - 1 + 127, 0) - down, 1)
    scale = np.exp2(byte - 127.0)
    codes = (blocks / scale).astype(np.float32).astype(dtype).astype(np.float64)
    return np.moveaxis((codes * scale).reshape(v.shape), -1, axis)


WIDE = False


def mx_kscale(k):
    if not WIDE:
        return np.ones(k)
    levels = np.array([10, -10, 5, -5, 0])
    if k % 512:
        return np.exp2(np.random.permutation(np.resize(levels, k // 32))).repeat(32)
    a = np.empty((k // 512, 16))
    for p in range(k // 512):
        a[p, :8] = np.random.permutation(np.resize(levels, 8))
        for g in range(8):
            far = levels[np.abs(levels - a[p, g]) >= 10]
            a[p, g + 8] = far[np.random.randint(len(far))]
    return np.exp2(a.ravel()).repeat(32)


def f64(x):
    return np.asarray(x).astype(np.float64)


def striped8(idx):
    return np.asarray(idx).reshape(8, -1, 16).transpose(0, 2, 1).reshape(128, -1).astype(np.uint16)


def unstriped8(offs):
    return offs.reshape(8, 16, -1).transpose(0, 2, 1).reshape(8, -1).astype(np.int64)


def pick8(x, idx, run):
    r = np.arange(len(x))
    return x[r[:, None], idx[r % (8 * run) // run]]


E2M1 = np.array([0.0, 0.5, 1.0, 1.5, 2.0, 3.0, 4.0, 6.0, -0.0, -0.5, -1.0, -1.5, -2.0, -3.0, -4.0, -6.0])


def pack_weight(w, fmt):
    k, n = w.shape
    w = f64(np.asarray(w, np.float32).astype(ml_dtypes.bfloat16)).reshape(k // 32, 32, n)
    amax = np.abs(w).max(1)
    if fmt == "e4m3":
        byte = np.frexp(amax)[1] - 1 + 127 - 7
    else:
        mant, ex = np.frexp(amax / 6.0)
        byte = np.where(mant > 0.5, ex, ex - 1) + 127
    byte = np.clip(np.where(amax > 0, byte, 1), 1, 254)
    scaled = (w * np.exp2(127.0 - byte)[:, None, :]).reshape(k, n).astype(np.float32)
    by_word = np.ascontiguousarray(scaled.reshape(k // 512, 128, 4, n).transpose(0, 1, 3, 2))
    if fmt == "e4m3":
        words = by_word.astype(ml_dtypes.float8_e4m3fn).view(np.uint8)
    else:
        c = by_word.astype(ml_dtypes.float4_e2m1fn).view(np.uint8) & 0xF
        words = (c[..., 0::2] | (c[..., 1::2] << 4)).reshape(k // 512, 128, 2 * n)
    return np.ascontiguousarray(words), np.ascontiguousarray(byte.astype(np.uint8).reshape(k // 512, 16, n))


def unpack_weight(words, scales, fmt):
    g, _, n = scales.shape
    words = np.ascontiguousarray(words).reshape(g, 128, n, -1)
    if fmt == "e4m3":
        vals = words.view(ml_dtypes.float8_e4m3fn).astype(np.float64)
    else:
        nib = np.empty((g, 128, n, 4), np.uint8)
        nib[..., 0::2] = words & 0xF
        nib[..., 1::2] = words >> 4
        vals = E2M1[nib]
    vals = vals * np.repeat(np.exp2(scales.astype(np.float64) - 127.0), 8, axis=1)[..., None]
    return vals.transpose(0, 1, 3, 2).reshape(g * 512, n)


C, D, I, Z, J, Q = 512, 512, 256, 512, 256, 128


def setup_inputs():
    n = np.random.standard_normal
    idx = np.stack([np.random.permutation(Z)[:I] for _ in range(8)])
    idx2 = np.stack([np.random.permutation(Z)[:J] for _ in range(8)])
    idx3 = np.stack([np.random.permutation(Z)[:J] for _ in range(8)])
    fc = mx_kscale(C)
    fd = mx_kscale(D)
    wpp = pack_weight(n((C, D)) * 1.0 / np.sqrt(C) * fc[:, None] / fd, "e4m3")
    oldsp = pack_weight(n((C, Z)) / fc[:, None], "e2m1")
    wkp = pack_weight(n((C, D)) * 1.0 / np.sqrt(C) * fc[:, None] / fd, "e2m1")
    newsp = pack_weight(n((C, I)) / fc[:, None], "e4m3")
    return {
        "wp_words": wpp[0],
        "wp_scales": wpp[1],
        "olds_words": oldsp[0],
        "olds_scales": oldsp[1],
        "wk_words": wkp[0],
        "wk_scales": wkp[1],
        "news_words": newsp[0],
        "news_scales": newsp[1],
        "query": (n((D, Q)) * 1.0 / np.sqrt(D) * fd[:, None]).astype(np.float32),
        "offs": striped8(idx),
        "offs2": striped8(idx2),
        "offs3": striped8(idx3),
    }


def reference(wp_words, wp_scales, olds_words, olds_scales, wk_words, wk_scales, news_words, news_scales, query, offs, offs2, offs3):
    idx = unstriped8(offs)
    idx2 = unstriped8(offs2)
    idx3 = unstriped8(offs3)
    wpu = unpack_weight(wp_words, wp_scales, "e4m3")
    oldsu = unpack_weight(olds_words, olds_scales, "e2m1")
    wku = unpack_weight(wk_words, wk_scales, "e2m1")
    newsu = unpack_weight(news_words, news_scales, "e4m3")
    kb = wpu.T @ oldsu
    kn = wku.T @ newsu
    f1 = np.zeros((D, Z))
    f1[np.arange(D)[:, None], idx[np.arange(D) % 512 // 64]] = kn
    pg = kb + f1
    queryq = mxq(f64(query), 0, "e4m3")
    pgq = mxq(pg, 0, "e4m3")
    s = queryq.T @ pgq
    y = pick8(s, idx2, 16) - pick8(s, idx3, 16)
    return y

@@ -1,0 +1,171 @@
+from contextlib import ExitStack
+
+import concourse.mybir as mybir
+
+F32 = mybir.dt.float32
+BF16 = mybir.dt.bfloat16
+I32 = mybir.dt.int32
+U32 = mybir.dt.uint32
+U16 = mybir.dt.uint16
+U8 = mybir.dt.uint8
+FP8X4 = mybir.dt.float8_e4m3fn_x4
+FP4X4 = mybir.dt.float4_e2m1fn_x4
+COPY = mybir.ActivationFunctionType.Copy
+ADD = mybir.AluOpType.add
+SUBTRACT = mybir.AluOpType.subtract
+
+P = 128
+C, D, I, Z, J, Q = 512, 512, 256, 512, 256, 128
+PLACES = 4
+BLOCKS = 16
+RUN = 8
+HALF_Z = Z // 2
+HALF_J = J // 2
+FLOPS = 2 * C * D * (Z + I) + 2 * D * Q * Z
+
+
+def tile_attend_headappend_plainq_kernel(tc, wp_words, wp_scales, olds_words, olds_scales, wk_words, wk_scales,
+                                          news_words, news_scales, query, offs, offs2, offs3, out):
+    nc = tc.nc
+    with ExitStack() as ctx:
+        lists = ctx.enter_context(tc.tile_pool(name="lists", bufs=1))
+        sb = ctx.enter_context(tc.tile_pool(name="sb", bufs=1))
+        psum = ctx.enter_context(tc.psum_pool(name="psum", bufs=1))
+
+        def tile(name, shape, dtype, tag=None):
+            return sb.tile(shape, dtype, name=name, tag=tag or name, align_bytes=64)
+
+        def load_words(queue, name, words, width):
+            t = tile(name, [P, width], U8)
+            queue.dma_start(out=t[:].bitcast(I32), in_=words.bitcast(I32))
+            return t
+
+        def load_plane(queues, name, scales, width):
+            t = tile(name, [P, width], U8)
+            rows = scales[0].bitcast(I32)
+            for g in range(4):
+                queues[g].dma_start(out=t[32 * g:32 * g + 4, :].bitcast(I32), in_=rows[4 * g:4 * g + 4, :])
+            return t
+
+        def load_scale_rows(queue, name, scales):
+            t = tile(name, [4, 4, D // 4], I32)
+            queue.dma_start(out=t[:], in_=scales[0].bitcast(I32).rearrange("(g r) n -> r g n", g=4))
+            return t
+
+        def deal_scales(name, rows):
+            t = tile(name, [P, D], U8, "dealt_scales")
+            words = t[:].bitcast(I32)
+            for g in range(4):
+                nc.vector.tensor_copy(
+                    out=words[32 * g:32 * g + 4, :].rearrange("r (t b m) -> r t b m", t=PLACES, b=BLOCKS),
+                    in_=rows[:, g, :].rearrange("r (b t m) -> r t b m", t=PLACES, b=BLOCKS))
+            return t
+
+        def deal(name, src, dtype):
+            width = src.shape[1]
+            t = tile(name, [P, width], U8, "dealt_words")
+            nc.vector.tensor_copy(
+                out=t[:].bitcast(dtype).rearrange("p (t b m) -> p t b m", t=PLACES, b=BLOCKS),
+                in_=src.bitcast(dtype).rearrange("p (b t m) -> p t b m", t=PLACES, b=BLOCKS))
+            return t
+
+        def load_list(name, src):
+            t = lists.tile([P, 16], U16, name=name)
+            nc.sync.dma_start(t[:], src)
+            return t
+
+        wk_rows = load_scale_rows(nc.sync, "wk_rows", wk_scales)
+        wk_raw = load_words(nc.scalar, "wk_raw", wk_words[0], 2 * D)
+        news = load_words(nc.sync, "news", news_words[0].rearrange("p n t -> p (n t)"), 4 * I)
+        news_s = load_plane((nc.scalar, nc.sync, nc.scalar, nc.sync), "news_s", news_scales, I)
+        put = load_list("put", offs)
+        wp_rows = load_scale_rows(nc.sync, "wp_rows", wp_scales)
+        wp_raw = load_words(nc.sync, "wp_raw", wp_words[0].rearrange("p n t -> p (n t)"), 4 * D)
+        olds = load_words(nc.sync, "olds", olds_words[0], 2 * Z)
+        olds_s = load_plane((nc.sync,) * 4, "olds_s", olds_scales, Z)
+
+        fresh = [tile("fresh%d" % t, [P, Z], F32) for t in range(PLACES)]
+        for t in range(PLACES):
+            nc.vector.memset(fresh[t][:], 0.0)
+        q_raw = tile("q_raw", [P, PLACES, Q], F32)
+        q_rows = query.rearrange("(b t m) q -> t b m q", t=PLACES, m=RUN)
+        for t in range(PLACES):
+            nc.sync.dma_start(out=q_raw[:, t, :], in_=q_rows[t])
+        pick_plus = load_list("pick_plus", offs2)
+        pick_minus = load_list("pick_minus", offs3)
+
+        wk = deal("wk", wk_raw[:], U16)
+        wk_s = deal_scales("wk_s", wk_rows)
+        widths = (I, I, 2 * I)
+        banks = [psum.tile([P, w], F32, name=n) for n, w in zip(("bank_a", "bank_b", "bank_c"), widths)]
+        kn = [tile("kn%d" % n, [P, w], F32) for n, w in enumerate(widths)]
+
+        def homes(a, b, c):
+            return [a[:], b[:], c[:, 0:I], c[:, I:2 * I]]
+
+        for t, ps in enumerate(homes(*banks)):
+            nc.tensor.matmul_mx(ps, lhsT=wk[:, 2 * P * t:2 * P * (t + 1)].bitcast(FP4X4),
+                                lhsT_scale=wk_s[:, P * t:P * (t + 1)], rhs=news[:].bitcast(FP8X4),
+                                rhs_scale=news_s[:], start=True, stop=True)
+        nc.scalar.activation(kn[0][:], banks[0][:], COPY)
+        for n in range(1, 3):
+            nc.vector.tensor_copy(out=kn[n][:], in_=banks[n][:])
+        for t, src in enumerate(homes(*kn)):
+            nc.scalar.activation(fresh[t][:].indirect(put[:]), src, COPY)
+
+        wp_s = deal_scales("wp_s", wp_rows)
+        wp = deal("wp", wp_raw[:], I32)
+        kb = [psum.tile([P, Z], F32, name="kb%d" % t) for t in range(PLACES)]
+        for t in range(PLACES):
+            nc.tensor.matmul_mx(kb[t][:], lhsT=wp[:, 4 * P * t:4 * P * (t + 1)].bitcast(FP8X4),
+                                lhsT_scale=wp_s[:, P * t:P * (t + 1)], rhs=olds[:].bitcast(FP4X4), rhs_scale=olds_s[:],
+                                start=True, stop=True)
+        kb_high = [tile("kb_high%d" % t, [P, HALF_Z], F32) for t in range(PLACES)]
+        for t in range(PLACES):
+            nc.vector.tensor_copy(out=kb_high[t][:], in_=kb[t][:, HALF_Z:Z])
+
+        pg_low = tile("pg_low", [P, HALF_Z, PLACES], BF16)
+        pg_high = tile("pg_high", [P, HALF_Z, PLACES], BF16)
+
+        def add_place(t):
+            nc.vector.tensor_tensor(pg_low[:, :, t], kb[t][:, 0:HALF_Z], fresh[t][:, 0:HALF_Z], ADD)
+            nc.gpsimd.tensor_tensor(pg_high[:, :, t], kb_high[t][:], fresh[t][:, HALF_Z:Z], ADD)
+
+        add_place(0)
+        q_bf = tile("q_bf", [P, Q, PLACES], BF16, "kb_high0")
+        nc.vector.tensor_copy(out=q_bf[:], in_=q_raw[:].rearrange("p t q -> p q t"))
+        q_codes = tile("q_codes", [P, Q], U32)
+        q_s = tile("q_s", [P, Q], U8)
+        nc.vector.quantize_mx(out=q_codes[:].bitcast(FP8X4), scales=q_s[:], in_=q_bf[:].rearrange("p q t -> p (q t)"))
+
+        for t in range(1, PLACES):
+            add_place(t)
+
+        s = tile("s", [P, Z], F32)
+        parts = [(pg_low, 0, 0, HALF_Z, "bank_c"), (pg_high, HALF_Z, 0, P, "bank_a"), (pg_high, HALF_Z, P, HALF_Z, "bank_b")]
+        for h, (pg, base, lo, hi, bank) in enumerate(parts):
+            codes = tile("pg_codes%d" % h, [P, hi - lo], U32)
+            scales = tile("pg_s%d" % h, [P, hi - lo], U8)
+            nc.vector.quantize_mx(out=codes[:].bitcast(FP8X4), scales=scales[:],
+                                  in_=pg[:, lo:hi, :].rearrange("p z t -> p (z t)"))
+            s_ps = psum.tile([P, hi - lo], F32, name=bank)
+            nc.tensor.matmul_mx(s_ps[:], lhsT=q_codes[:].bitcast(FP8X4), lhsT_scale=q_s[:],
+                                rhs=codes[:].bitcast(FP8X4), rhs_scale=scales[:], start=True, stop=True)
+            cols = s[:, base + lo:base + hi]
+            if h == 1:
+                nc.vector.tensor_copy(out=cols, in_=s_ps[:])
+            else:
+                nc.scalar.copy(out=cols, in_=s_ps[:])
+
+        halves = []
+        for h in range(2):
+            cols = slice(h * HALF_J // 16, (h + 1) * HALF_J // 16)
+            plus = tile("plus%d" % h, [P, HALF_J], F32)
+            minus = tile("minus%d" % h, [P, HALF_J], F32)
+            nc.vector.tensor_copy(plus[:], s[:].indirect(pick_plus[:, cols]))
+            nc.scalar.activation(minus[:], s[:].indirect(pick_minus[:, cols]), COPY)
+            halves.append((plus, minus))
+        for h, (plus, minus) in enumerate(halves):
+            y = tile("y%d" % h, [P, HALF_J], F32)
+            nc.vector.tensor_tensor(y[:], plus[:], minus[:], SUBTRACT)
+            (nc.sync, nc.scalar)[h].dma_start(out=out[:, h * HALF_J:(h + 1) * HALF_J], in_=y[:])

@@ -19,6 +19,8 @@ C, D, I, Z, J, Q = 512, 512, 256, 512, 256, 128
 PLACES = 4
 BLOCKS = 16
 RUN = 8
+QUADRANTS = 4
+LIST_ROWS = 16
 HALF_Z = Z // 2
 HALF_J = J // 2
 FLOPS = 2 * C * D * (Z + I) + 2 * D * Q * Z
@@ -36,53 +38,53 @@ def tile_attend_headappend_plainq_kernel(tc, wp_words, wp_scales, olds_words, ol
             return sb.tile(shape, dtype, name=name, tag=tag or name, align_bytes=64)
 
         def load_words(queue, name, words, width):
-            t = tile(name, [P, width], U8)
-            queue.dma_start(out=t[:].bitcast(I32), in_=words.bitcast(I32))
-            return t
+            loaded = tile(name, [P, width], U8)
+            queue.dma_start(out=loaded[:].bitcast(I32), in_=words.bitcast(I32))
+            return loaded
 
-        def load_plane(queues, name, scales, width):
-            t = tile(name, [P, width], U8)
+        def load_scales(queues, name, scales, width):
+            loaded = tile(name, [P, width], U8)
             rows = scales[0].bitcast(I32)
-            for g in range(4):
-                queues[g].dma_start(out=t[32 * g:32 * g + 4, :].bitcast(I32), in_=rows[4 * g:4 * g + 4, :])
-            return t
+            for g in range(QUADRANTS):
+                queues[g].dma_start(out=loaded[32 * g:32 * g + 4, :].bitcast(I32), in_=rows[4 * g:4 * g + 4, :])
+            return loaded
 
         def load_scale_rows(queue, name, scales):
-            t = tile(name, [4, 4, D // 4], I32)
-            queue.dma_start(out=t[:], in_=scales[0].bitcast(I32).rearrange("(g r) n -> r g n", g=4))
-            return t
+            loaded = tile(name, [4, QUADRANTS, D // 4], I32)
+            queue.dma_start(out=loaded[:], in_=scales[0].bitcast(I32).rearrange("(g r) n -> r g n", g=QUADRANTS))
+            return loaded
 
         def deal_scales(name, rows):
-            t = tile(name, [P, D], U8, "dealt_scales")
-            words = t[:].bitcast(I32)
-            for g in range(4):
+            dealt = tile(name, [P, D], U8)
+            words = dealt[:].bitcast(I32)
+            for g in range(QUADRANTS):
                 nc.vector.tensor_copy(
                     out=words[32 * g:32 * g + 4, :].rearrange("r (t b m) -> r t b m", t=PLACES, b=BLOCKS),
                     in_=rows[:, g, :].rearrange("r (b t m) -> r t b m", t=PLACES, b=BLOCKS))
-            return t
+            return dealt
 
-        def deal(name, src, dtype):
-            width = src.shape[1]
-            t = tile(name, [P, width], U8, "dealt_words")
-            nc.vector.tensor_copy(
-                out=t[:].bitcast(dtype).rearrange("p (t b m) -> p t b m", t=PLACES, b=BLOCKS),
-                in_=src.bitcast(dtype).rearrange("p (b t m) -> p t b m", t=PLACES, b=BLOCKS))
-            return t
+        def deal_words(name, given, dtype):
+            dealt = tile(name, [P, given.shape[1]], U8, "dealt_words")
+            to = dealt[:].bitcast(dtype).rearrange("p (t b m) -> p t b m", t=PLACES, b=BLOCKS)
+            source = given.bitcast(dtype).rearrange("p (b t m) -> p t b m", t=PLACES, b=BLOCKS)
+            for places in (slice(0, 2), slice(2, 4)):
+                nc.vector.tensor_copy(out=to[:, places], in_=source[:, places])
+            return dealt
 
-        def load_list(name, src):
-            t = lists.tile([P, 16], U16, name=name)
-            nc.sync.dma_start(t[:], src)
-            return t
+        def load_list(name, offsets):
+            loaded = lists.tile([P, offsets.shape[1]], U16, name=name)
+            nc.sync.dma_start(loaded[:], offsets)
+            return loaded
 
         wk_rows = load_scale_rows(nc.sync, "wk_rows", wk_scales)
         wk_raw = load_words(nc.scalar, "wk_raw", wk_words[0], 2 * D)
         news = load_words(nc.sync, "news", news_words[0].rearrange("p n t -> p (n t)"), 4 * I)
-        news_s = load_plane((nc.scalar, nc.sync, nc.scalar, nc.sync), "news_s", news_scales, I)
+        news_s = load_scales((nc.scalar, nc.sync, nc.scalar, nc.sync), "news_s", news_scales, I)
         put = load_list("put", offs)
         wp_rows = load_scale_rows(nc.sync, "wp_rows", wp_scales)
         wp_raw = load_words(nc.sync, "wp_raw", wp_words[0].rearrange("p n t -> p (n t)"), 4 * D)
         olds = load_words(nc.sync, "olds", olds_words[0], 2 * Z)
-        olds_s = load_plane((nc.sync,) * 4, "olds_s", olds_scales, Z)
+        olds_s = load_scales((nc.sync,) * QUADRANTS, "olds_s", olds_scales, Z)
 
         fresh = [tile("fresh%d" % t, [P, Z], F32) for t in range(PLACES)]
         for t in range(PLACES):
@@ -94,27 +96,33 @@ def tile_attend_headappend_plainq_kernel(tc, wp_words, wp_scales, olds_words, ol
         pick_plus = load_list("pick_plus", offs2)
         pick_minus = load_list("pick_minus", offs3)
 
-        wk = deal("wk", wk_raw[:], U16)
         wk_s = deal_scales("wk_s", wk_rows)
+        wk = deal_words("wk", wk_raw[:], U16)
         widths = (I, I, 2 * I)
         banks = [psum.tile([P, w], F32, name=n) for n, w in zip(("bank_a", "bank_b", "bank_c"), widths)]
         kn = [tile("kn%d" % n, [P, w], F32) for n, w in enumerate(widths)]
 
-        def homes(a, b, c):
-            return [a[:], b[:], c[:, 0:I], c[:, I:2 * I]]
+        def by_place(first, second, last_two):
+            return [first[:], second[:], last_two[:, 0:I], last_two[:, I:2 * I]]
 
-        for t, ps in enumerate(homes(*banks)):
-            nc.tensor.matmul_mx(ps, lhsT=wk[:, 2 * P * t:2 * P * (t + 1)].bitcast(FP4X4),
+        for t, kn_ps in enumerate(by_place(*banks)):
+            nc.tensor.matmul_mx(kn_ps, lhsT=wk[:, 2 * P * t:2 * P * (t + 1)].bitcast(FP4X4),
                                 lhsT_scale=wk_s[:, P * t:P * (t + 1)], rhs=news[:].bitcast(FP8X4),
                                 rhs_scale=news_s[:], start=True, stop=True)
         nc.scalar.activation(kn[0][:], banks[0][:], COPY)
-        for n in range(1, 3):
-            nc.vector.tensor_copy(out=kn[n][:], in_=banks[n][:])
-        for t, src in enumerate(homes(*kn)):
-            nc.scalar.activation(fresh[t][:].indirect(put[:]), src, COPY)
+        nc.vector.tensor_copy(out=kn[1][:], in_=banks[1][:])
+
+        def scatter(t):
+            nc.scalar.activation(fresh[t][:].indirect(put[:]), by_place(*kn)[t], COPY)
+
+        scatter(0)
+        scatter(1)
 
         wp_s = deal_scales("wp_s", wp_rows)
-        wp = deal("wp", wp_raw[:], I32)
+        wp = deal_words("wp", wp_raw[:], I32)
+        nc.vector.tensor_copy(out=kn[2][:], in_=banks[2][:])
+        scatter(2)
+        scatter(3)
         kb = [psum.tile([P, Z], F32, name="kb%d" % t) for t in range(PLACES)]
         for t in range(PLACES):
             nc.tensor.matmul_mx(kb[t][:], lhsT=wp[:, 4 * P * t:4 * P * (t + 1)].bitcast(FP8X4),
@@ -142,28 +150,28 @@ def tile_attend_headappend_plainq_kernel(tc, wp_words, wp_scales, olds_words, ol
             add_place(t)
 
         s = tile("s", [P, Z], F32)
-        parts = [(pg_low, 0, 0, HALF_Z, "bank_c"), (pg_high, HALF_Z, 0, P, "bank_a"), (pg_high, HALF_Z, P, HALF_Z, "bank_b")]
-        for h, (pg, base, lo, hi, bank) in enumerate(parts):
-            codes = tile("pg_codes%d" % h, [P, hi - lo], U32)
-            scales = tile("pg_s%d" % h, [P, hi - lo], U8)
+        parts = [(pg_low, 0, 0, HALF_Z, "bank_c"), (pg_high, HALF_Z, 0, P, "bank_a"),
+                 (pg_high, HALF_Z, P, HALF_Z, "bank_b")]
+        for n, (pg, base, lo, hi, bank) in enumerate(parts):
+            codes = tile("pg_codes%d" % n, [P, hi - lo], U32)
+            scales = tile("pg_s%d" % n, [P, hi - lo], U8)
             nc.vector.quantize_mx(out=codes[:].bitcast(FP8X4), scales=scales[:],
                                   in_=pg[:, lo:hi, :].rearrange("p z t -> p (z t)"))
             s_ps = psum.tile([P, hi - lo], F32, name=bank)
             nc.tensor.matmul_mx(s_ps[:], lhsT=q_codes[:].bitcast(FP8X4), lhsT_scale=q_s[:],
                                 rhs=codes[:].bitcast(FP8X4), rhs_scale=scales[:], start=True, stop=True)
-            cols = s[:, base + lo:base + hi]
-            if h == 1:
-                nc.vector.tensor_copy(out=cols, in_=s_ps[:])
+            if n % 2 == 1:
+                nc.vector.tensor_copy(out=s[:, base + lo:base + hi], in_=s_ps[:])
             else:
-                nc.scalar.copy(out=cols, in_=s_ps[:])
+                nc.scalar.copy(out=s[:, base + lo:base + hi], in_=s_ps[:])
 
         halves = []
         for h in range(2):
-            cols = slice(h * HALF_J // 16, (h + 1) * HALF_J // 16)
+            entries = slice(h * HALF_J // LIST_ROWS, (h + 1) * HALF_J // LIST_ROWS)
             plus = tile("plus%d" % h, [P, HALF_J], F32)
             minus = tile("minus%d" % h, [P, HALF_J], F32)
-            nc.vector.tensor_copy(plus[:], s[:].indirect(pick_plus[:, cols]))
-            nc.scalar.activation(minus[:], s[:].indirect(pick_minus[:, cols]), COPY)
+            nc.vector.tensor_copy(plus[:], s[:].indirect(pick_plus[:, entries]))
+            nc.scalar.activation(minus[:], s[:].indirect(pick_minus[:, entries]), COPY)
             halves.append((plus, minus))
         for h, (plus, minus) in enumerate(halves):
             y = tile("y%d" % h, [P, HALF_J], F32)

from contextlib import ExitStack

import concourse.mybir as mybir

F32 = mybir.dt.float32
BF16 = mybir.dt.bfloat16
I32 = mybir.dt.int32
U32 = mybir.dt.uint32
U16 = mybir.dt.uint16
U8 = mybir.dt.uint8
FP8X4 = mybir.dt.float8_e4m3fn_x4
FP4X4 = mybir.dt.float4_e2m1fn_x4
COPY = mybir.ActivationFunctionType.Copy
ADD = mybir.AluOpType.add
SUBTRACT = mybir.AluOpType.subtract

P = 128
C, D, I, Z, J, Q = 512, 512, 256, 512, 256, 128
PLACES = 4
BLOCKS = 16
RUN = 8
QUADRANTS = 4
LIST_ROWS = 16
HALF_Z = Z // 2
HALF_J = J // 2
FLOPS = 2 * C * D * (Z + I) + 2 * D * Q * Z


def tile_attend_headappend_plainq_kernel(tc, wp_words, wp_scales, olds_words, olds_scales, wk_words, wk_scales,
                                          news_words, news_scales, query, offs, offs2, offs3, out):
    nc = tc.nc
    with ExitStack() as ctx:
        lists = ctx.enter_context(tc.tile_pool(name="lists", bufs=1))
        sb = ctx.enter_context(tc.tile_pool(name="sb", bufs=1))
        psum = ctx.enter_context(tc.psum_pool(name="psum", bufs=1))

        def tile(name, shape, dtype, tag=None):
            return sb.tile(shape, dtype, name=name, tag=tag or name, align_bytes=64)

        def load_words(queue, name, words, width):
            loaded = tile(name, [P, width], U8)
            queue.dma_start(out=loaded[:].bitcast(I32), in_=words.bitcast(I32))
            return loaded

        def load_scales(queues, name, scales, width):
            loaded = tile(name, [P, width], U8)
            rows = scales[0].bitcast(I32)
            for g in range(QUADRANTS):
                queues[g].dma_start(out=loaded[32 * g:32 * g + 4, :].bitcast(I32), in_=rows[4 * g:4 * g + 4, :])
            return loaded

        def load_scale_rows(queue, name, scales):
            loaded = tile(name, [4, QUADRANTS, D // 4], I32)
            queue.dma_start(out=loaded[:], in_=scales[0].bitcast(I32).rearrange("(g r) n -> r g n", g=QUADRANTS))
            return loaded

        def deal_scales(name, rows):
            dealt = tile(name, [P, D], U8)
            words = dealt[:].bitcast(I32)
            for g in range(QUADRANTS):
                nc.vector.tensor_copy(
                    out=words[32 * g:32 * g + 4, :].rearrange("r (t b m) -> r t b m", t=PLACES, b=BLOCKS),
                    in_=rows[:, g, :].rearrange("r (b t m) -> r t b m", t=PLACES, b=BLOCKS))
            return dealt

        def deal_words(name, given, dtype):
            dealt = tile(name, [P, given.shape[1]], U8, "dealt_words")
            to = dealt[:].bitcast(dtype).rearrange("p (t b m) -> p t b m", t=PLACES, b=BLOCKS)
            source = given.bitcast(dtype).rearrange("p (b t m) -> p t b m", t=PLACES, b=BLOCKS)
            for places in (slice(0, 2), slice(2, 4)):
                nc.vector.tensor_copy(out=to[:, places], in_=source[:, places])
            return dealt

        def load_list(name, offsets):
            loaded = lists.tile([P, offsets.shape[1]], U16, name=name)
            nc.sync.dma_start(loaded[:], offsets)
            return loaded

        wk_rows = load_scale_rows(nc.sync, "wk_rows", wk_scales)
        wk_raw = load_words(nc.scalar, "wk_raw", wk_words[0], 2 * D)
        news = load_words(nc.sync, "news", news_words[0].rearrange("p n t -> p (n t)"), 4 * I)
        news_s = load_scales((nc.scalar, nc.sync, nc.scalar, nc.sync), "news_s", news_scales, I)
        put = load_list("put", offs)
        wp_rows = load_scale_rows(nc.sync, "wp_rows", wp_scales)
        wp_raw = load_words(nc.sync, "wp_raw", wp_words[0].rearrange("p n t -> p (n t)"), 4 * D)
        olds = load_words(nc.sync, "olds", olds_words[0], 2 * Z)
        olds_s = load_scales((nc.sync,) * QUADRANTS, "olds_s", olds_scales, Z)

        fresh = [tile("fresh%d" % t, [P, Z], F32) for t in range(PLACES)]
        for t in range(PLACES):
            nc.vector.memset(fresh[t][:], 0.0)
        q_raw = tile("q_raw", [P, PLACES, Q], F32)
        q_rows = query.rearrange("(b t m) q -> t b m q", t=PLACES, m=RUN)
        for t in range(PLACES):
            nc.sync.dma_start(out=q_raw[:, t, :], in_=q_rows[t])
        pick_plus = load_list("pick_plus", offs2)
        pick_minus = load_list("pick_minus", offs3)

        wk_s = deal_scales("wk_s", wk_rows)
        wk = deal_words("wk", wk_raw[:], U16)
        widths = (I, I, 2 * I)
        banks = [psum.tile([P, w], F32, name=n) for n, w in zip(("bank_a", "bank_b", "bank_c"), widths)]
        kn = [tile("kn%d" % n, [P, w], F32) for n, w in enumerate(widths)]

        def by_place(first, second, last_two):
            return [first[:], second[:], last_two[:, 0:I], last_two[:, I:2 * I]]

        for t, kn_ps in enumerate(by_place(*banks)):
            nc.tensor.matmul_mx(kn_ps, lhsT=wk[:, 2 * P * t:2 * P * (t + 1)].bitcast(FP4X4),
                                lhsT_scale=wk_s[:, P * t:P * (t + 1)], rhs=news[:].bitcast(FP8X4),
                                rhs_scale=news_s[:], start=True, stop=True)
        nc.scalar.activation(kn[0][:], banks[0][:], COPY)
        nc.vector.tensor_copy(out=kn[1][:], in_=banks[1][:])

        def scatter(t):
            nc.scalar.activation(fresh[t][:].indirect(put[:]), by_place(*kn)[t], COPY)

        scatter(0)
        scatter(1)

        wp_s = deal_scales("wp_s", wp_rows)
        wp = deal_words("wp", wp_raw[:], I32)
        nc.vector.tensor_copy(out=kn[2][:], in_=banks[2][:])
        scatter(2)
        scatter(3)
        kb = [psum.tile([P, Z], F32, name="kb%d" % t) for t in range(PLACES)]
        for t in range(PLACES):
            nc.tensor.matmul_mx(kb[t][:], lhsT=wp[:, 4 * P * t:4 * P * (t + 1)].bitcast(FP8X4),
                                lhsT_scale=wp_s[:, P * t:P * (t + 1)], rhs=olds[:].bitcast(FP4X4), rhs_scale=olds_s[:],
                                start=True, stop=True)
        kb_high = [tile("kb_high%d" % t, [P, HALF_Z], F32) for t in range(PLACES)]
        for t in range(PLACES):
            nc.vector.tensor_copy(out=kb_high[t][:], in_=kb[t][:, HALF_Z:Z])

        pg_low = tile("pg_low", [P, HALF_Z, PLACES], BF16)
        pg_high = tile("pg_high", [P, HALF_Z, PLACES], BF16)

        def add_place(t):
            nc.vector.tensor_tensor(pg_low[:, :, t], kb[t][:, 0:HALF_Z], fresh[t][:, 0:HALF_Z], ADD)
            nc.gpsimd.tensor_tensor(pg_high[:, :, t], kb_high[t][:], fresh[t][:, HALF_Z:Z], ADD)

        add_place(0)
        q_bf = tile("q_bf", [P, Q, PLACES], BF16, "kb_high0")
        nc.vector.tensor_copy(out=q_bf[:], in_=q_raw[:].rearrange("p t q -> p q t"))
        q_codes = tile("q_codes", [P, Q], U32)
        q_s = tile("q_s", [P, Q], U8)
        nc.vector.quantize_mx(out=q_codes[:].bitcast(FP8X4), scales=q_s[:], in_=q_bf[:].rearrange("p q t -> p (q t)"))

        for t in range(1, PLACES):
            add_place(t)

        s = tile("s", [P, Z], F32)
        parts = [(pg_low, 0, 0, HALF_Z, "bank_c"), (pg_high, HALF_Z, 0, P, "bank_a"),
                 (pg_high, HALF_Z, P, HALF_Z, "bank_b")]
        for n, (pg, base, lo, hi, bank) in enumerate(parts):
            codes = tile("pg_codes%d" % n, [P, hi - lo], U32)
            scales = tile("pg_s%d" % n, [P, hi - lo], U8)
            nc.vector.quantize_mx(out=codes[:].bitcast(FP8X4), scales=scales[:],
                                  in_=pg[:, lo:hi, :].rearrange("p z t -> p (z t)"))
            s_ps = psum.tile([P, hi - lo], F32, name=bank)
            nc.tensor.matmul_mx(s_ps[:], lhsT=q_codes[:].bitcast(FP8X4), lhsT_scale=q_s[:],
                                rhs=codes[:].bitcast(FP8X4), rhs_scale=scales[:], start=True, stop=True)
            if n % 2 == 1:
                nc.vector.tensor_copy(out=s[:, base + lo:base + hi], in_=s_ps[:])
            else:
                nc.scalar.copy(out=s[:, base + lo:base + hi], in_=s_ps[:])

        halves = []
        for h in range(2):
            entries = slice(h * HALF_J // LIST_ROWS, (h + 1) * HALF_J // LIST_ROWS)
            plus = tile("plus%d" % h, [P, HALF_J], F32)
            minus = tile("minus%d" % h, [P, HALF_J], F32)
            nc.vector.tensor_copy(plus[:], s[:].indirect(pick_plus[:, entries]))
            nc.scalar.activation(minus[:], s[:].indirect(pick_minus[:, entries]), COPY)
            halves.append((plus, minus))
        for h, (plus, minus) in enumerate(halves):
            y = tile("y%d" % h, [P, HALF_J], F32)
            nc.vector.tensor_tensor(y[:], plus[:], minus[:], SUBTRACT)
            (nc.sync, nc.scalar)[h].dma_start(out=out[:, h * HALF_J:(h + 1) * HALF_J], in_=y[:])
